import numpy as np
import ml_dtypes


def mxq(x, axis, fmt="e4m3"):
    dtype, down = {"e4m3": (ml_dtypes.float8_e4m3fn, 7), "e5m2": (ml_dtypes.float8_e5m2, 14)}[fmt]
    v = np.moveaxis(np.asarray(x, np.float32).astype(ml_dtypes.bfloat16).astype(np.float64), axis, -1)
    blocks = v.reshape(v.shape[:-1] + (-1, 32))
    amax = np.abs(blocks).max(-1, keepdims=True)
    byte = np.maximum(np.where(amax > 0, np.frexp(amax)[1] - 1 + 127, 0) - down, 1)
    scale = np.exp2(byte - 127.0)
    codes = (blocks / scale).astype(np.float32).astype(dtype).astype(np.float64)
    return np.moveaxis((codes * scale).reshape(v.shape), -1, axis)


WIDE = False


def mx_kscale(k):
    if not WIDE:
        return np.ones(k)
    levels = np.array([24, -24, 12, -12, 0])
    if k % 512:
        return np.exp2(np.random.permutation(np.resize(levels, k // 32))).repeat(32)
    a = np.empty((k // 512, 16))
    for p in range(k // 512):
        a[p, :8] = np.random.permutation(np.resize(levels, 8))
        for g in range(8):
            far = levels[np.abs(levels - a[p, g]) >= 10]
            a[p, g + 8] = far[np.random.randint(len(far))]
    return np.exp2(a.ravel()).repeat(32)


def f64(x):
    return np.asarray(x).astype(np.float64)


def striped8(idx):
    return np.concatenate([v.reshape(-1, 16).T for v in idx]).astype(np.uint16)


def unstriped8(offs):
    return np.stack([offs[16 * g:16 * g + 16].T.reshape(-1) for g in range(8)]).astype(np.int64)


E2M1 = np.array([0.0, 0.5, 1.0, 1.5, 2.0, 3.0, 4.0, 6.0, -0.0, -0.5, -1.0, -1.5, -2.0, -3.0, -4.0, -6.0])


def pack_weight(w, fmt):
    k, n = w.shape
    w = f64(np.asarray(w, np.float32).astype(ml_dtypes.bfloat16)).reshape(k // 32, 32, n)
    amax = np.abs(w).max(1)
    if fmt == "e4m3":
        byte = np.frexp(amax)[1] - 1 + 127 - 7
    else:
        mant, ex = np.frexp(amax / 6.0)
        byte = np.where(mant > 0.5, ex, ex - 1) + 127
    byte = np.clip(np.where(amax > 0, byte, 1), 1, 254)
    scaled = (w * np.exp2(127.0 - byte)[:, None, :]).reshape(k, n).astype(np.float32)
    by_word = np.ascontiguousarray(scaled.reshape(k // 512, 128, 4, n).transpose(0, 1, 3, 2))
    if fmt == "e4m3":
        words = by_word.astype(ml_dtypes.float8_e4m3fn).view(np.uint8)
    else:
        c = by_word.astype(ml_dtypes.float4_e2m1fn).view(np.uint8) & 0xF
        words = (c[..., 0::2] | (c[..., 1::2] << 4)).reshape(k // 512, 128, 2 * n)
    return np.ascontiguousarray(words), np.ascontiguousarray(byte.astype(np.uint8).reshape(k // 512, 16, n))


def unpack_weight(words, scales, fmt):
    g, _, n = scales.shape
    words = np.ascontiguousarray(words).reshape(g, 128, n, -1)
    if fmt == "e4m3":
        vals = words.view(ml_dtypes.float8_e4m3fn).astype(np.float64)
    else:
        nib = np.empty((g, 128, n, 4), np.uint8)
        nib[..., 0::2] = words & 0xF
        nib[..., 1::2] = words >> 4
        vals = E2M1[nib]
    vals = vals * np.repeat(np.exp2(scales.astype(np.float64) - 127.0), 8, axis=1)[..., None]
    return vals.transpose(0, 1, 3, 2).reshape(g * 512, n)


def planes(y):
    n, m = y.shape
    v = y.astype(np.float32).astype(ml_dtypes.bfloat16).astype(np.float64).reshape(n // 32, 32, m)
    top = np.abs(v).max(1)
    byte = np.clip(np.where(top > 0, np.frexp(top)[1] - 1 + 127 - 7, 1), 1, 254)
    codes = (v * np.exp2(127.0 - byte)[:, None, :]).reshape(n, m).astype(np.float32).astype(ml_dtypes.float8_e4m3fn).view(np.uint8)
    words = codes.reshape(n // 512, 128, 4, m).transpose(0, 1, 3, 2)
    return np.ascontiguousarray(words), np.ascontiguousarray(byte.astype(np.uint8).reshape(n // 512, 16, m))


def silu(f):
    return f / (1.0 + np.exp(-np.maximum(f, -700.0)))


K, L, N, T, J = 512, 512, 512, 2048, 1024


def setup_inputs():
    n = np.random.standard_normal
    s = mx_kscale(K)[:, None]
    s2 = mx_kscale(L)[:, None]
    p_wb = pack_weight(n((L, N)) / np.sqrt(L) / s2, "e2m1")
    return {
        "xT": (n((K, T)) * s).astype(np.float32),
        "wgt": np.repeat(np.random.uniform(0.5, 2.0, (8, J)), 16, axis=0).astype(np.float32),
        "zT": (n((L, T)) * s2).astype(np.float32),
        "wgt2": np.repeat(np.random.uniform(0.5, 2.0, (8, J)), 16, axis=0).astype(np.float32),
        "wa": (n((K, N)) / np.sqrt(K) / s).astype(np.float32),
        "wb_words": p_wb[0],
        "wb_scales": p_wb[1],
        "b": (0.3 * n(N)).astype(np.float32),
        "offs": striped8(np.stack([np.random.permutation(T)[:J] for _ in range(8)])),
        "offs2": striped8(np.stack([np.random.permutation(T)[:J] for _ in range(8)])),
    }


def reference(xT, wgt, zT, wgt2, wa, wb_words, wb_scales, b, offs, offs2):
    idx = unstriped8(offs)
    idx2 = unstriped8(offs2)
    rows = np.arange(K)
    xg = f64(wgt)[rows // 4 % 128] * f64(xT)[rows[:, None], idx[rows % 512 // 64]]
    xT_ = mxq(xg, 0, "e4m3")
    rows = np.arange(L)
    xg = f64(wgt2)[rows // 4 % 128] * f64(zT)[rows[:, None], idx2[rows % 512 // 64]]
    zT_ = mxq(xg, 0, "e4m3")
    wa_ = mxq(f64(wa), 0, "e4m3")
    wb_ = unpack_weight(wb_words, wb_scales, "e2m1")
    ya = wa_.T @ xT_
    yb = wb_.T @ zT_
    out_0 = silu(ya) * yb + f64(b)[:, None]
    return (out_0,) + planes(out_0)

@@ -1,0 +1,217 @@
+from contextlib import ExitStack
+
+import concourse.mybir as mybir
+
+K, N, T, J = 512, 512, 2048, 1024
+FLOPS = 2 * 2 * K * N * J
+
+F32 = mybir.dt.float32
+BF16 = mybir.dt.bfloat16
+I32 = mybir.dt.int32
+U32 = mybir.dt.uint32
+U16 = mybir.dt.uint16
+U8 = mybir.dt.uint8
+FP8X4 = mybir.dt.float8_e4m3fn_x4
+FP4X4 = mybir.dt.float4_e2m1fn_x4
+MULT = mybir.AluOpType.mult
+ADD = mybir.AluOpType.add
+SILU = mybir.ActivationFunctionType.Silu
+IDENTITY = mybir.ActivationFunctionType.Identity
+
+P = 128
+PACK = 4
+LIST_ROWS = 16
+BANK = 512
+X_CHUNKS = [256, 256, 256, 256]
+Z_CHUNKS = [256, 256, 256, 128, 128]
+BIAS_ENGINES = "ssvv"
+WA_ON_VECTOR = 64
+
+
+def spans(widths):
+    return [slice(sum(widths[:c]), sum(widths[: c + 1])) for c in range(len(widths))]
+
+
+def tile_list_glu_biasP_kernel(
+    tc, xT, wgt, zT, wgt2, wa, wb_words, wb_scales, b, offs, offs2, out_0, out_1, out_2
+):
+    nc = tc.nc
+    with ExitStack() as ctx:
+        keep = ctx.enter_context(tc.tile_pool(name="keep", bufs=1))
+        ring = ctx.enter_context(tc.tile_pool(name="ring", bufs=4))
+        psum = ctx.enter_context(tc.psum_pool(name="psum", bufs=8))
+
+        def sb(name, shape, dtype):
+            return keep.tile(shape, dtype, name=name, align_bytes=64)
+
+        def load_big(rows):
+            plane = ring.tile([P, T], F32, name="plane")
+            nc.sync.dma_start(out=plane[:], in_=rows)
+            return plane
+
+        def gather(picked, plane, i, offsets, weights, cols):
+            nc.vector.tensor_tensor(
+                picked[:, i, :],
+                plane[:].indirect(offsets[:, cols.start // LIST_ROWS : cols.stop // LIST_ROWS]),
+                weights[:, cols],
+                MULT,
+            )
+
+        def interleave(name, rows):
+            width = rows.shape[2]
+            packed = sb(name, [P, width * PACK], BF16)
+            nc.scalar.copy(
+                out=packed[:].rearrange("p (c e i) -> p c i e", e=4, i=PACK),
+                in_=rows[:].rearrange("p i (c e) -> p c i e", e=4),
+            )
+            return packed
+
+        def quantize(packed, codes, scales):
+            nc.vector.quantize_mx(out=codes.bitcast(FP8X4), scales=scales, in_=packed[:])
+
+        def quantize_new(name, packed):
+            width = packed.shape[1] // PACK
+            codes = sb(name + "_codes", [P, width], U32)
+            scales = sb(name + "_scales", [P, width], U8)
+            quantize(packed, codes[:], scales[:])
+            return codes, scales
+
+        def project(codes, scales, w_slice, w_scales):
+            width = codes.shape[1]
+            per_bank = BANK // width
+            banks = []
+            for t0 in range(0, PACK, per_bank):
+                bank = psum.tile([P, per_bank, width], F32, name="bank")
+                for u in range(per_bank):
+                    t = t0 + u
+                    nc.tensor.matmul_mx(
+                        out=bank[:, u, :],
+                        lhsT=w_slice(t),
+                        lhsT_scale=w_scales[:, P * t : P * (t + 1)],
+                        rhs=codes[:].bitcast(FP8X4),
+                        rhs_scale=scales[:],
+                        start=True,
+                        stop=True,
+                    )
+                banks.append((slice(t0, t0 + per_bank), bank))
+            return banks
+
+        x_list = keep.tile([P, J // LIST_ROWS], U16, name="x_list")
+        z_list = keep.tile([P, J // LIST_ROWS], U16, name="z_list")
+        x_wgt = sb("x_wgt", [P, J], F32)
+        z_wgt = sb("z_wgt", [P, J], F32)
+        wb_raw = sb("wb_raw", [P, 2 * N], U8)
+        wb_raw_scales = sb("wb_raw_scales", [P, N], U8)
+        bias = sb("bias", [P, PACK], F32)
+        x_rows = xT.rearrange("(p i) t -> i p t", i=PACK)
+        z_rows = zT.rearrange("(p i) t -> i p t", i=PACK)
+        halves = spans([J // 2, J // 2])
+        x_cols = spans(X_CHUNKS)
+        z_cols = spans(Z_CHUNKS)
+
+        nc.vector.memset(wb_raw_scales[:].bitcast(U32), 0)
+        for q in range(4):
+            nc.scalar.dma_start(
+                out=wb_raw_scales[32 * q : 32 * q + 4, :].bitcast(I32),
+                in_=wb_scales[0, 4 * q : 4 * q + 4, :].bitcast(I32),
+            )
+        nc.scalar.dma_start(out=bias[:], in_=b.rearrange("(p t) -> p t", t=PACK))
+        nc.scalar.dma_start(out=wb_raw[:].bitcast(I32), in_=wb_words[0].bitcast(I32))
+
+        nc.sync.dma_start(x_list[:], offs)
+        x_plane = [load_big(x_rows[0])]
+        for cols in halves:
+            nc.sync.dma_start(out=x_wgt[:, cols], in_=wgt[:, cols])
+        for i in range(1, PACK):
+            x_plane.append(load_big(x_rows[i]))
+        nc.sync.dma_start(z_list[:], offs2)
+        nc.sync.dma_start(out=z_wgt[:, halves[0]], in_=wgt2[:, halves[0]])
+
+        warm = sb("warm", [P, 1], F32)
+        nc.scalar.activation(out=warm[:], in_=bias[:, 0:1], func=SILU)
+
+        wb_codes = sb("wb_codes", [P, 2 * N], U8)
+        wb_scale_plane = sb("wb_scale_plane", [P, N], U8)
+        nc.vector.tensor_copy(
+            out=wb_codes[:].rearrange("p (t m e) -> p m t e", t=PACK, e=2),
+            in_=wb_raw[:].rearrange("p (m t e) -> p m t e", t=PACK, e=2),
+        )
+        nc.vector.tensor_copy(
+            out=wb_scale_plane[:].rearrange("p (t m) -> p m t", t=PACK),
+            in_=wb_raw_scales[:].rearrange("p (m t) -> p m t", t=PACK),
+        )
+
+        x_picked = [sb("x_picked%d" % c, [P, PACK, w], F32) for c, w in enumerate(X_CHUNKS)]
+        for i in range(PACK):
+            for c, cols in enumerate(x_cols):
+                gather(x_picked[c], x_plane[i], i, x_list, x_wgt, cols)
+        x_packed = [interleave("x_packed%d" % c, x_picked[c]) for c in range(len(X_CHUNKS))]
+        x_mx = [quantize_new("x%d" % c, x_packed[c]) for c in range(len(X_CHUNKS))]
+
+        z_plane = [load_big(z_rows[0])]
+        nc.sync.dma_start(out=z_wgt[:, halves[1]], in_=wgt2[:, halves[1]])
+        wa_raw = load_big(wa.rearrange("(p i) n -> p (i n)", i=PACK))
+        z_plane.append(load_big(z_rows[1]))
+        z_plane.append(load_big(z_rows[2]))
+        z_picked = [sb("z_picked%d" % c, [P, PACK, w], F32) for c, w in enumerate(Z_CHUNKS)]
+        for c, cols in enumerate(z_cols):
+            gather(z_picked[c], z_plane[0], 0, z_list, z_wgt, cols)
+        z_plane.append(load_big(z_rows[3]))
+
+        wa_packed = sb("wa_packed", [P, N * PACK], BF16)
+        wa_to = wa_packed[:].rearrange("p (t m i) -> p m i t", t=PACK, i=PACK)
+        wa_from = wa_raw[:].rearrange("p (i m t) -> p m i t", i=PACK, t=PACK)
+        nc.vector.tensor_copy(out=wa_to[:, :WA_ON_VECTOR], in_=wa_from[:, :WA_ON_VECTOR])
+        nc.scalar.copy(out=wa_to[:, WA_ON_VECTOR:], in_=wa_from[:, WA_ON_VECTOR:])
+        wa_codes, wa_scales = quantize_new("wa", wa_packed)
+
+        gate = sb("gate", [P, PACK, J], F32)
+        for cols, (codes, scales) in zip(x_cols, x_mx):
+            ya = project(codes, scales, lambda t: wa_codes[:, P * t : P * (t + 1)].bitcast(FP8X4), wa_scales)
+            for ts, bank in ya:
+                nc.scalar.activation(out=gate[:, ts, cols], in_=bank[:], func=SILU)
+
+        for i in range(1, PACK):
+            for c, cols in enumerate(z_cols):
+                gather(z_picked[c], z_plane[i], i, z_list, z_wgt, cols)
+        z_packed = [interleave("z_packed%d" % c, z_picked[c]) for c in range(len(Z_CHUNKS))]
+
+        out_rows = out_0.rearrange("(p t) j -> p t j", t=PACK)
+        out_words = out_1[0].rearrange("p j i -> p (j i)").bitcast(I32)
+        out_scales = sb("out_scales", [P, J], U8)
+        for c, cols in enumerate(z_cols):
+            width = Z_CHUNKS[c]
+            codes, scales = quantize_new("z%d" % c, z_packed[c])
+            yb = project(
+                codes, scales, lambda t: wb_codes[:, 2 * P * t : 2 * P * (t + 1)].bitcast(FP4X4), wb_scale_plane
+            )
+            product = sb("product%d" % c, [P, PACK, width], F32)
+            result = sb("result%d" % c, [P, PACK, width], F32)
+            for ts, bank in yb:
+                nc.vector.tensor_tensor(product[:, ts, :], bank[:], gate[:, ts, cols], MULT)
+            for t in range(PACK):
+                if BIAS_ENGINES[t] == "s":
+                    nc.scalar.activation(
+                        out=result[:, t, :], in_=product[:, t, :], func=IDENTITY, bias=bias[:, t : t + 1]
+                    )
+                elif BIAS_ENGINES[t] == "g":
+                    nc.gpsimd.tensor_scalar(
+                        result[:, t, :], product[:, t, :], 1.0, bias[:, t : t + 1], MULT, ADD
+                    )
+                else:
+                    nc.vector.tensor_scalar(
+                        result[:, t, :], product[:, t, :], bias[:, t : t + 1], None, ADD
+                    )
+            nc.sync.dma_start(out=out_rows[:, :, cols], in_=result[:])
+
+            rounded = interleave("rounded%d" % c, result)
+            words = sb("words%d" % c, [P, width], U32)
+            quantize(rounded, words[:], out_scales[:, cols])
+            nc.sync.dma_start(out=out_words[:, cols], in_=words[:].bitcast(I32))
+
+        for q in range(4):
+            queue = nc.sync if q % 2 == 0 else nc.scalar
+            queue.dma_start(
+                out=out_2[0, 4 * q : 4 * q + 4, :].bitcast(I32),
+                in_=out_scales[32 * q : 32 * q + 4, :].bitcast(I32),
+            )

@@ -22,10 +22,10 @@ P = 128
 PACK = 4
 LIST_ROWS = 16
 BANK = 512
-X_CHUNKS = [256, 256, 256, 256]
+X_CHUNKS = [256, 256, 512]
 Z_CHUNKS = [256, 256, 256, 128, 128]
-BIAS_ENGINES = "ssvv"
-WA_ON_VECTOR = 64
+BIAS_ENGINES = "svvv"
+PLANE_LAG = 2
 
 
 def spans(widths):
@@ -51,7 +51,7 @@ def tile_list_glu_biasP_kernel(
 
         def gather(picked, plane, i, offsets, weights, cols):
             nc.vector.tensor_tensor(
-                picked[:, i, :],
+                picked[:, i, cols],
                 plane[:].indirect(offsets[:, cols.start // LIST_ROWS : cols.stop // LIST_ROWS]),
                 weights[:, cols],
                 MULT,
@@ -61,8 +61,8 @@ def tile_list_glu_biasP_kernel(
             width = rows.shape[2]
             packed = sb(name, [P, width * PACK], BF16)
             nc.scalar.copy(
-                out=packed[:].rearrange("p (c e i) -> p c i e", e=4, i=PACK),
-                in_=rows[:].rearrange("p i (c e) -> p c i e", e=4),
+                out=packed[:].rearrange("p (c e i) -> p c i e", e=2, i=PACK),
+                in_=rows.rearrange("p i (c e) -> p c i e", e=2),
             )
             return packed
 
@@ -106,22 +106,22 @@ def tile_list_glu_biasP_kernel(
         x_rows = xT.rearrange("(p i) t -> i p t", i=PACK)
         z_rows = zT.rearrange("(p i) t -> i p t", i=PACK)
         halves = spans([J // 2, J // 2])
+        whole = spans([J])
         x_cols = spans(X_CHUNKS)
         z_cols = spans(Z_CHUNKS)
 
-        nc.vector.memset(wb_raw_scales[:].bitcast(U32), 0)
+        nc.gpsimd.memset(wb_raw_scales[:].bitcast(U32), 0)
+        nc.sync.dma_start(x_list[:], offs)
+        nc.sync.dma_start(out=wb_raw[:].bitcast(I32), in_=wb_words[0].bitcast(I32))
+        nc.sync.dma_start(out=bias[:], in_=b.rearrange("(p t) -> p t", t=PACK))
+        x_plane = [load_big(x_rows[0])]
+        nc.sync.dma_start(out=x_wgt[:, halves[0]], in_=wgt[:, halves[0]])
         for q in range(4):
-            nc.scalar.dma_start(
+            nc.sync.dma_start(
                 out=wb_raw_scales[32 * q : 32 * q + 4, :].bitcast(I32),
                 in_=wb_scales[0, 4 * q : 4 * q + 4, :].bitcast(I32),
             )
-        nc.scalar.dma_start(out=bias[:], in_=b.rearrange("(p t) -> p t", t=PACK))
-        nc.scalar.dma_start(out=wb_raw[:].bitcast(I32), in_=wb_words[0].bitcast(I32))
-
-        nc.sync.dma_start(x_list[:], offs)
-        x_plane = [load_big(x_rows[0])]
-        for cols in halves:
-            nc.sync.dma_start(out=x_wgt[:, cols], in_=wgt[:, cols])
+        nc.sync.dma_start(out=x_wgt[:, halves[1]], in_=wgt[:, halves[1]])
         for i in range(1, PACK):
             x_plane.append(load_big(x_rows[i]))
         nc.sync.dma_start(z_list[:], offs2)
@@ -133,19 +133,19 @@ def tile_list_glu_biasP_kernel(
         wb_codes = sb("wb_codes", [P, 2 * N], U8)
         wb_scale_plane = sb("wb_scale_plane", [P, N], U8)
         nc.vector.tensor_copy(
-            out=wb_codes[:].rearrange("p (t m e) -> p m t e", t=PACK, e=2),
-            in_=wb_raw[:].rearrange("p (m t e) -> p m t e", t=PACK, e=2),
+            out=wb_codes[:].rearrange("p (t m e) -> p t m e", t=PACK, e=2),
+            in_=wb_raw[:].rearrange("p (m t e) -> p t m e", t=PACK, e=2),
         )
         nc.vector.tensor_copy(
-            out=wb_scale_plane[:].rearrange("p (t m) -> p m t", t=PACK),
-            in_=wb_raw_scales[:].rearrange("p (m t) -> p m t", t=PACK),
+            out=wb_scale_plane[:].rearrange("p (t m) -> p t m", t=PACK),
+            in_=wb_raw_scales[:].rearrange("p (m t) -> p t m", t=PACK),
         )
 
-        x_picked = [sb("x_picked%d" % c, [P, PACK, w], F32) for c, w in enumerate(X_CHUNKS)]
-        for i in range(PACK):
-            for c, cols in enumerate(x_cols):
-                gather(x_picked[c], x_plane[i], i, x_list, x_wgt, cols)
-        x_packed = [interleave("x_packed%d" % c, x_picked[c]) for c in range(len(X_CHUNKS))]
+        x_picked = sb("x_picked", [P, PACK, J], F32)
+        for i, pieces in enumerate([halves, whole, whole, x_cols]):
+            for cols in pieces:
+                gather(x_picked, x_plane[i], i, x_list, x_wgt, cols)
+        x_packed = [interleave("x_packed%d" % c, x_picked[:, :, cols]) for c, cols in enumerate(x_cols)]
         x_mx = [quantize_new("x%d" % c, x_packed[c]) for c in range(len(X_CHUNKS))]
 
         z_plane = [load_big(z_rows[0])]
@@ -153,16 +153,16 @@ def tile_list_glu_biasP_kernel(
         wa_raw = load_big(wa.rearrange("(p i) n -> p (i n)", i=PACK))
         z_plane.append(load_big(z_rows[1]))
         z_plane.append(load_big(z_rows[2]))
-        z_picked = [sb("z_picked%d" % c, [P, PACK, w], F32) for c, w in enumerate(Z_CHUNKS)]
-        for c, cols in enumerate(z_cols):
-            gather(z_picked[c], z_plane[0], 0, z_list, z_wgt, cols)
+        z_picked = sb("z_picked", [P, PACK, J], F32)
+        for cols in halves:
+            gather(z_picked, z_plane[0], 0, z_list, z_wgt, cols)
         z_plane.append(load_big(z_rows[3]))
 
         wa_packed = sb("wa_packed", [P, N * PACK], BF16)
         wa_to = wa_packed[:].rearrange("p (t m i) -> p m i t", t=PACK, i=PACK)
         wa_from = wa_raw[:].rearrange("p (i m t) -> p m i t", i=PACK, t=PACK)
-        nc.vector.tensor_copy(out=wa_to[:, :WA_ON_VECTOR], in_=wa_from[:, :WA_ON_VECTOR])
-        nc.scalar.copy(out=wa_to[:, WA_ON_VECTOR:], in_=wa_from[:, WA_ON_VECTOR:])
+        nc.vector.tensor_copy(out=wa_to[:, :, :, :2], in_=wa_from[:, :, :, :2])
+        nc.scalar.copy(out=wa_to[:, :, :, 2:], in_=wa_from[:, :, :, 2:])
         wa_codes, wa_scales = quantize_new("wa", wa_packed)
 
         gate = sb("gate", [P, PACK, J], F32)
@@ -171,20 +171,32 @@ def tile_list_glu_biasP_kernel(
             for ts, bank in ya:
                 nc.scalar.activation(out=gate[:, ts, cols], in_=bank[:], func=SILU)
 
-        for i in range(1, PACK):
-            for c, cols in enumerate(z_cols):
-                gather(z_picked[c], z_plane[i], i, z_list, z_wgt, cols)
-        z_packed = [interleave("z_packed%d" % c, z_picked[c]) for c in range(len(Z_CHUNKS))]
+        for i, pieces in ((1, whole), (2, whole), (3, z_cols)):
+            for cols in pieces:
+                gather(z_picked, z_plane[i], i, z_list, z_wgt, cols)
+        z_packed = [interleave("z_packed%d" % c, z_picked[:, :, cols]) for c, cols in enumerate(z_cols)]
 
         out_rows = out_0.rearrange("(p t) j -> p t j", t=PACK)
         out_words = out_1[0].rearrange("p j i -> p (j i)").bitcast(I32)
+        rounded = []
         out_scales = sb("out_scales", [P, J], U8)
+
+        def emit_planes(c):
+            words = sb("words%d" % c, [P, Z_CHUNKS[c]], U32)
+            quantize(rounded[c], words[:], out_scales[:, z_cols[c]])
+            nc.sync.dma_start(out=out_words[:, z_cols[c]], in_=words[:].bitcast(I32))
+
+        yb_banks = []
+        for c in range(len(Z_CHUNKS)):
+            codes, scales = quantize_new("z%d" % c, z_packed[c])
+            yb_banks.append(
+                project(
+                    codes, scales, lambda t: wb_codes[:, 2 * P * t : 2 * P * (t + 1)].bitcast(FP4X4), wb_scale_plane
+                )
+            )
         for c, cols in enumerate(z_cols):
             width = Z_CHUNKS[c]
-            codes, scales = quantize_new("z%d" % c, z_packed[c])
-            yb = project(
-                codes, scales, lambda t: wb_codes[:, 2 * P * t : 2 * P * (t + 1)].bitcast(FP4X4), wb_scale_plane
-            )
+            yb = yb_banks[c]
             product = sb("product%d" % c, [P, PACK, width], F32)
             result = sb("result%d" % c, [P, PACK, width], F32)
             for ts, bank in yb:
@@ -204,10 +216,11 @@ def tile_list_glu_biasP_kernel(
                     )
             nc.sync.dma_start(out=out_rows[:, :, cols], in_=result[:])
 
-            rounded = interleave("rounded%d" % c, result)
-            words = sb("words%d" % c, [P, width], U32)
-            quantize(rounded, words[:], out_scales[:, cols])
-            nc.sync.dma_start(out=out_words[:, cols], in_=words[:].bitcast(I32))
+            rounded.append(interleave("rounded%d" % c, result[:]))
+            if c >= PLANE_LAG:
+                emit_planes(c - PLANE_LAG)
+        for c in range(len(Z_CHUNKS) - PLANE_LAG, len(Z_CHUNKS)):
+            emit_planes(c)
 
         for q in range(4):
             queue = nc.sync if q % 2 == 0 else nc.scalar

@@ -113,7 +113,6 @@ def tile_list_glu_biasP_kernel(
         nc.gpsimd.memset(wb_raw_scales[:].bitcast(U32), 0)
         nc.sync.dma_start(x_list[:], offs)
         nc.sync.dma_start(out=wb_raw[:].bitcast(I32), in_=wb_words[0].bitcast(I32))
-        nc.sync.dma_start(out=bias[:], in_=b.rearrange("(p t) -> p t", t=PACK))
         x_plane = [load_big(x_rows[0])]
         nc.sync.dma_start(out=x_wgt[:, halves[0]], in_=wgt[:, halves[0]])
         for q in range(4):
@@ -125,10 +124,8 @@ def tile_list_glu_biasP_kernel(
         for i in range(1, PACK):
             x_plane.append(load_big(x_rows[i]))
         nc.sync.dma_start(z_list[:], offs2)
+        nc.sync.dma_start(out=bias[:], in_=b.rearrange("(p t) -> p t", t=PACK))
         nc.sync.dma_start(out=z_wgt[:, halves[0]], in_=wgt2[:, halves[0]])
-
-        warm = sb("warm", [P, 1], F32)
-        nc.scalar.activation(out=warm[:], in_=bias[:, 0:1], func=SILU)
 
         wb_codes = sb("wb_codes", [P, 2 * N], U8)
         wb_scale_plane = sb("wb_scale_plane", [P, N], U8)

from contextlib import ExitStack

import concourse.mybir as mybir

K, N, T, J = 512, 512, 2048, 1024
FLOPS = 2 * 2 * K * N * J

F32 = mybir.dt.float32
BF16 = mybir.dt.bfloat16
I32 = mybir.dt.int32
U32 = mybir.dt.uint32
U16 = mybir.dt.uint16
U8 = mybir.dt.uint8
FP8X4 = mybir.dt.float8_e4m3fn_x4
FP4X4 = mybir.dt.float4_e2m1fn_x4
MULT = mybir.AluOpType.mult
ADD = mybir.AluOpType.add
SILU = mybir.ActivationFunctionType.Silu
IDENTITY = mybir.ActivationFunctionType.Identity

P = 128
PACK = 4
LIST_ROWS = 16
BANK = 512
X_CHUNKS = [256, 256, 512]
Z_CHUNKS = [256, 256, 256, 128, 128]
BIAS_ENGINES = "svvv"
PLANE_LAG = 2


def spans(widths):
    return [slice(sum(widths[:c]), sum(widths[: c + 1])) for c in range(len(widths))]


def tile_list_glu_biasP_kernel(
    tc, xT, wgt, zT, wgt2, wa, wb_words, wb_scales, b, offs, offs2, out_0, out_1, out_2
):
    nc = tc.nc
    with ExitStack() as ctx:
        keep = ctx.enter_context(tc.tile_pool(name="keep", bufs=1))
        ring = ctx.enter_context(tc.tile_pool(name="ring", bufs=4))
        psum = ctx.enter_context(tc.psum_pool(name="psum", bufs=8))

        def sb(name, shape, dtype):
            return keep.tile(shape, dtype, name=name, align_bytes=64)

        def load_big(rows):
            plane = ring.tile([P, T], F32, name="plane")
            nc.sync.dma_start(out=plane[:], in_=rows)
            return plane

        def gather(picked, plane, i, offsets, weights, cols):
            nc.vector.tensor_tensor(
                picked[:, i, cols],
                plane[:].indirect(offsets[:, cols.start // LIST_ROWS : cols.stop // LIST_ROWS]),
                weights[:, cols],
                MULT,
            )

        def interleave(name, rows):
            width = rows.shape[2]
            packed = sb(name, [P, width * PACK], BF16)
            nc.scalar.copy(
                out=packed[:].rearrange("p (c e i) -> p c i e", e=2, i=PACK),
                in_=rows.rearrange("p i (c e) -> p c i e", e=2),
            )
            return packed

        def quantize(packed, codes, scales):
            nc.vector.quantize_mx(out=codes.bitcast(FP8X4), scales=scales, in_=packed[:])

        def quantize_new(name, packed):
            width = packed.shape[1] // PACK
            codes = sb(name + "_codes", [P, width], U32)
            scales = sb(name + "_scales", [P, width], U8)
            quantize(packed, codes[:], scales[:])
            return codes, scales

        def project(codes, scales, w_slice, w_scales):
            width = codes.shape[1]
            per_bank = BANK // width
            banks = []
            for t0 in range(0, PACK, per_bank):
                bank = psum.tile([P, per_bank, width], F32, name="bank")
                for u in range(per_bank):
                    t = t0 + u
                    nc.tensor.matmul_mx(
                        out=bank[:, u, :],
                        lhsT=w_slice(t),
                        lhsT_scale=w_scales[:, P * t : P * (t + 1)],
                        rhs=codes[:].bitcast(FP8X4),
                        rhs_scale=scales[:],
                        start=True,
                        stop=True,
                    )
                banks.append((slice(t0, t0 + per_bank), bank))
            return banks

        x_list = keep.tile([P, J // LIST_ROWS], U16, name="x_list")
        z_list = keep.tile([P, J // LIST_ROWS], U16, name="z_list")
        x_wgt = sb("x_wgt", [P, J], F32)
        z_wgt = sb("z_wgt", [P, J], F32)
        wb_raw = sb("wb_raw", [P, 2 * N], U8)
        wb_raw_scales = sb("wb_raw_scales", [P, N], U8)
        bias = sb("bias", [P, PACK], F32)
        x_rows = xT.rearrange("(p i) t -> i p t", i=PACK)
        z_rows = zT.rearrange("(p i) t -> i p t", i=PACK)
        halves = spans([J // 2, J // 2])
        whole = spans([J])
        x_cols = spans(X_CHUNKS)
        z_cols = spans(Z_CHUNKS)

        nc.gpsimd.memset(wb_raw_scales[:].bitcast(U32), 0)
        nc.sync.dma_start(x_list[:], offs)
        nc.sync.dma_start(out=wb_raw[:].bitcast(I32), in_=wb_words[0].bitcast(I32))
        x_plane = [load_big(x_rows[0])]
        nc.sync.dma_start(out=x_wgt[:, halves[0]], in_=wgt[:, halves[0]])
        for q in range(4):
            nc.sync.dma_start(
                out=wb_raw_scales[32 * q : 32 * q + 4, :].bitcast(I32),
                in_=wb_scales[0, 4 * q : 4 * q + 4, :].bitcast(I32),
            )
        nc.sync.dma_start(out=x_wgt[:, halves[1]], in_=wgt[:, halves[1]])
        for i in range(1, PACK):
            x_plane.append(load_big(x_rows[i]))
        nc.sync.dma_start(z_list[:], offs2)
        nc.sync.dma_start(out=bias[:], in_=b.rearrange("(p t) -> p t", t=PACK))
        nc.sync.dma_start(out=z_wgt[:, halves[0]], in_=wgt2[:, halves[0]])

        wb_codes = sb("wb_codes", [P, 2 * N], U8)
        wb_scale_plane = sb("wb_scale_plane", [P, N], U8)
        nc.vector.tensor_copy(
            out=wb_codes[:].rearrange("p (t m e) -> p t m e", t=PACK, e=2),
            in_=wb_raw[:].rearrange("p (m t e) -> p t m e", t=PACK, e=2),
        )
        nc.vector.tensor_copy(
            out=wb_scale_plane[:].rearrange("p (t m) -> p t m", t=PACK),
            in_=wb_raw_scales[:].rearrange("p (m t) -> p t m", t=PACK),
        )

        x_picked = sb("x_picked", [P, PACK, J], F32)
        for i, pieces in enumerate([halves, whole, whole, x_cols]):
            for cols in pieces:
                gather(x_picked, x_plane[i], i, x_list, x_wgt, cols)
        x_packed = [interleave("x_packed%d" % c, x_picked[:, :, cols]) for c, cols in enumerate(x_cols)]
        x_mx = [quantize_new("x%d" % c, x_packed[c]) for c in range(len(X_CHUNKS))]

        z_plane = [load_big(z_rows[0])]
        nc.sync.dma_start(out=z_wgt[:, halves[1]], in_=wgt2[:, halves[1]])
        wa_raw = load_big(wa.rearrange("(p i) n -> p (i n)", i=PACK))
        z_plane.append(load_big(z_rows[1]))
        z_plane.append(load_big(z_rows[2]))
        z_picked = sb("z_picked", [P, PACK, J], F32)
        for cols in halves:
            gather(z_picked, z_plane[0], 0, z_list, z_wgt, cols)
        z_plane.append(load_big(z_rows[3]))

        wa_packed = sb("wa_packed", [P, N * PACK], BF16)
        wa_to = wa_packed[:].rearrange("p (t m i) -> p m i t", t=PACK, i=PACK)
        wa_from = wa_raw[:].rearrange("p (i m t) -> p m i t", i=PACK, t=PACK)
        nc.vector.tensor_copy(out=wa_to[:, :, :, :2], in_=wa_from[:, :, :, :2])
        nc.scalar.copy(out=wa_to[:, :, :, 2:], in_=wa_from[:, :, :, 2:])
        wa_codes, wa_scales = quantize_new("wa", wa_packed)

        gate = sb("gate", [P, PACK, J], F32)
        for cols, (codes, scales) in zip(x_cols, x_mx):
            ya = project(codes, scales, lambda t: wa_codes[:, P * t : P * (t + 1)].bitcast(FP8X4), wa_scales)
            for ts, bank in ya:
                nc.scalar.activation(out=gate[:, ts, cols], in_=bank[:], func=SILU)

        for i, pieces in ((1, whole), (2, whole), (3, z_cols)):
            for cols in pieces:
                gather(z_picked, z_plane[i], i, z_list, z_wgt, cols)
        z_packed = [interleave("z_packed%d" % c, z_picked[:, :, cols]) for c, cols in enumerate(z_cols)]

        out_rows = out_0.rearrange("(p t) j -> p t j", t=PACK)
        out_words = out_1[0].rearrange("p j i -> p (j i)").bitcast(I32)
        rounded = []
        out_scales = sb("out_scales", [P, J], U8)

        def emit_planes(c):
            words = sb("words%d" % c, [P, Z_CHUNKS[c]], U32)
            quantize(rounded[c], words[:], out_scales[:, z_cols[c]])
            nc.sync.dma_start(out=out_words[:, z_cols[c]], in_=words[:].bitcast(I32))

        yb_banks = []
        for c in range(len(Z_CHUNKS)):
            codes, scales = quantize_new("z%d" % c, z_packed[c])
            yb_banks.append(
                project(
                    codes, scales, lambda t: wb_codes[:, 2 * P * t : 2 * P * (t + 1)].bitcast(FP4X4), wb_scale_plane
                )
            )
        for c, cols in enumerate(z_cols):
            width = Z_CHUNKS[c]
            yb = yb_banks[c]
            product = sb("product%d" % c, [P, PACK, width], F32)
            result = sb("result%d" % c, [P, PACK, width], F32)
            for ts, bank in yb:
                nc.vector.tensor_tensor(product[:, ts, :], bank[:], gate[:, ts, cols], MULT)
            for t in range(PACK):
                if BIAS_ENGINES[t] == "s":
                    nc.scalar.activation(
                        out=result[:, t, :], in_=product[:, t, :], func=IDENTITY, bias=bias[:, t : t + 1]
                    )
                elif BIAS_ENGINES[t] == "g":
                    nc.gpsimd.tensor_scalar(
                        result[:, t, :], product[:, t, :], 1.0, bias[:, t : t + 1], MULT, ADD
                    )
                else:
                    nc.vector.tensor_scalar(
                        result[:, t, :], product[:, t, :], bias[:, t : t + 1], None, ADD
                    )
            nc.sync.dma_start(out=out_rows[:, :, cols], in_=result[:])

            rounded.append(interleave("rounded%d" % c, result[:]))
            if c >= PLANE_LAG:
                emit_planes(c - PLANE_LAG)
        for c in range(len(Z_CHUNKS) - PLANE_LAG, len(Z_CHUNKS)):
            emit_planes(c)

        for q in range(4):
            queue = nc.sync if q % 2 == 0 else nc.scalar
            queue.dma_start(
                out=out_2[0, 4 * q : 4 * q + 4, :].bitcast(I32),
                in_=out_scales[32 * q : 32 * q + 4, :].bitcast(I32),
            )
